import numpy as np
import ml_dtypes


def mxq(x, axis, fmt="e4m3"):
    dtype, down = {"e4m3": (ml_dtypes.float8_e4m3fn, 7), "e5m2": (ml_dtypes.float8_e5m2, 14)}[fmt]
    v = np.moveaxis(np.asarray(x, np.float32).astype(ml_dtypes.bfloat16).astype(np.float64), axis, -1)
    blocks = v.reshape(v.shape[:-1] + (-1, 32))
    amax = np.abs(blocks).max(-1, keepdims=True)
    byte = np.maximum(np.where(amax > 0, np.frexp(amax)[1] - 1 + 127, 0) - down, 1)
    scale = np.exp2(byte - 127.0)
    codes = (blocks / scale).astype(np.float32).astype(dtype).astype(np.float64)
    return np.moveaxis((codes * scale).reshape(v.shape), -1, axis)


WIDE = False


def mx_kscale(k):
    if not WIDE:
        return np.ones(k)
    levels = np.array([10, -10, 5, -5, 0])
    if k % 512:
        return np.exp2(np.random.permutation(np.resize(levels, k // 32))).repeat(32)
    a = np.empty((k // 512, 16))
    for p in range(k // 512):
        a[p, :8] = np.random.permutation(np.resize(levels, 8))
        for g in range(8):
            far = levels[np.abs(levels - a[p, g]) >= 10]
            a[p, g + 8] = far[np.random.randint(len(far))]
    return np.exp2(a.ravel()).repeat(32)


BF16 = ml_dtypes.bfloat16


def bf(x):
    return np.asarray(x, np.float32).astype(BF16)


def f64(x):
    return np.asarray(x).astype(np.float64)


E2M1 = np.array([0.0, 0.5, 1.0, 1.5, 2.0, 3.0, 4.0, 6.0, -0.0, -0.5, -1.0, -1.5, -2.0, -3.0, -4.0, -6.0])


def pack_weight(w, fmt):
    k, n = w.shape
    w = f64(bf(w)).reshape(k // 32, 32, n)
    amax = np.abs(w).max(1)
    if fmt == "e4m3":
        byte = np.frexp(amax)[1] - 1 + 127 - 7
    else:
        mant, ex = np.frexp(amax / 6.0)
        byte = np.where(mant > 0.5, ex, ex - 1) + 127
    byte = np.clip(np.where(amax > 0, byte, 1), 1, 254)
    scaled = (w * np.exp2(127.0 - byte)[:, None, :]).reshape(k, n).astype(np.float32)
    by_word = np.ascontiguousarray(scaled.reshape(k // 512, 128, 4, n).transpose(0, 1, 3, 2))
    if fmt == "e4m3":
        words = by_word.astype(ml_dtypes.float8_e4m3fn).view(np.uint8)
    else:
        c = by_word.astype(ml_dtypes.float4_e2m1fn).view(np.uint8) & 0xF
        words = c[..., 0::2] | (c[..., 1::2] << 4)
    return np.ascontiguousarray(words), np.ascontiguousarray(byte.astype(np.uint8).reshape(k // 512, 16, n))


def unpack_weight(words, scales, fmt):
    g, p, n, _ = words.shape
    if fmt == "e4m3":
        vals = np.ascontiguousarray(words).view(ml_dtypes.float8_e4m3fn).astype(np.float64)
    else:
        nib = np.empty((g, p, n, 4), np.uint8)
        nib[..., 0::2] = words & 0xF
        nib[..., 1::2] = words >> 4
        vals = E2M1[nib]
    vals = vals * np.repeat(np.exp2(scales.astype(np.float64) - 127.0), 8, axis=1)[..., None]
    return vals.transpose(0, 1, 3, 2).reshape(g * 512, n)
def pack4(w):
    words, scales = pack_weight(w, "e2m1")
    return words.reshape(words.shape[0], 128, -1), scales


def unpack4(words, scales):
    return unpack_weight(words.reshape(words.shape[0], 128, -1, 2), scales, "e2m1")


def planes(Y):
    n, m = Y.shape
    b = f64(bf(Y)).reshape(n // 32, 32, m)
    amax = np.abs(b).max(1)
    byte = np.clip(np.where(amax > 0, np.frexp(amax)[1] - 1 + 127 - 7, 1), 1, 254)
    codes = (b * np.exp2(127.0 - byte)[:, None, :]).reshape(n, m).astype(np.float32).astype(ml_dtypes.float8_e4m3fn).view(np.uint8)
    words = codes.reshape(n // 512, 128, 4, m).transpose(0, 1, 3, 2)
    return np.ascontiguousarray(words), np.ascontiguousarray(byte.astype(np.uint8).reshape(n // 512, 16, m))


M, S, A, K, F, N = 1536, 768, 256, 1024, 1536, 1024

def setup_inputs():
    s = mx_kscale(K)
    t = mx_kscale(F)
    state = np.random.randn(M, S)
    action = np.tanh(np.random.randn(M, A))
    x = np.concatenate([state, action], axis=1)
    w1 = np.random.randn(K, F) / np.sqrt(K)
    b1 = 0.3 * np.random.randn(F)
    w2 = np.random.randn(F, N) * np.sqrt(2.0 / F)
    b2 = 0.3 * np.random.randn(N)
    baseline = 0.4 + 0.1 * np.random.randn(N)
    value_w = np.sign(np.random.randn(N)) * np.exp(0.8 * np.random.randn(N))
    x_words, x_scales = pack_weight(x.T * s[:, None], "e4m3")
    w1_words, w1_scales = pack4(w1 / s[:, None] * t[None, :])
    return {"x_words": x_words, "x_scales": x_scales,
            "w1_words": w1_words, "w1_scales": w1_scales,
            "b1": bf(b1 * t), "w2": bf(w2 / t[:, None]), "b2": bf(b2),
            "baseline": bf(baseline), "value_w": bf(value_w)}

def reference(x_words, x_scales, w1_words, w1_scales, b1, w2, b2, baseline, value_w):
    XT = unpack_weight(x_words, x_scales, "e4m3")
    W1 = unpack4(w1_words, w1_scales)
    H = np.maximum((XT.T @ W1) + f64(b1), 0.0)
    Z = mxq(H, 1, "e4m3") @ mxq(f64(w2), 0, "e4m3")
    y = (np.maximum(Z + f64(b2), 0.0) - f64(baseline)) * f64(value_w)
    Y = y.T
    words, scales = planes(Y)
    return y, words, scales

@@ -1,0 +1,268 @@
+from contextlib import ExitStack
+
+import concourse.mybir as mybir
+from concourse.masks import make_identity
+
+M, K, F, N = 1536, 1024, 1536, 1024
+FLOPS = 2 * M * K * F + 2 * M * F * N
+
+F32 = mybir.dt.float32
+BF16 = mybir.dt.bfloat16
+I32 = mybir.dt.int32
+U32 = mybir.dt.uint32
+U8 = mybir.dt.uint8
+FP8X4 = mybir.dt.float8_e4m3fn_x4
+FP4X4 = mybir.dt.float4_e2m1fn_x4
+ACT = mybir.ActivationFunctionType
+ALU = mybir.AluOpType
+
+P = 128
+PACK = 4
+GROUP = P * PACK
+CHUNK = 512
+K_PASSES = K // GROUP
+F_GROUPS = F // GROUP
+N_GROUPS = N // GROUP
+CHUNKS = M // CHUNK
+QUADS = 4
+
+
+def tile_critic_value_contributions_h2_kernel(
+    tc, x_words, x_scales, w1_words, w1_scales, b1, w2, b2, baseline, value_w, out_0, out_1, out_2
+):
+    nc = tc.nc
+    with ExitStack() as ctx:
+        keep = ctx.enter_context(tc.tile_pool(name="keep", bufs=1))
+        work = ctx.enter_context(tc.tile_pool(name="work", bufs=3))
+        psum = ctx.enter_context(tc.psum_pool(name="psum", bufs=8))
+        ctx.enter_context(tc.manual_schedule())
+
+        def kept(shape, dtype, name):
+            return keep.tile(shape, dtype, name=name, align_bytes=64)
+
+        w1s_raw = kept([P, K_PASSES, F], U8, "w1s_raw")
+        xs = kept([P, K_PASSES, M], U8, "xs")
+        nc.vector.memset(w1s_raw[:].bitcast(I32), 0)
+        nc.vector.memset(xs[:].bitcast(I32), 0)
+
+        def load_scale_rows(plane, rows, q):
+            nc.sync.dma_start(
+                out=plane[32 * q : 32 * q + 4, :, :].bitcast(I32),
+                in_=rows[:, 4 * q : 4 * q + 4, :].rearrange("k r n -> r k n").bitcast(I32),
+            )
+
+        w1_raw = [kept([P, K_PASSES, 2 * GROUP], U8, "w1_raw%d" % g) for g in range(F_GROUPS)]
+        xw = [kept([P, K_PASSES, CHUNK], U32, "xw%d" % c) for c in range(CHUNKS)]
+        w2_raw = [kept([P, PACK, N], BF16, "w2_raw%d" % g) for g in range(F_GROUPS)]
+
+        def load_w1(eng, g):
+            eng.dma_start(
+                out=w1_raw[g][:].bitcast(I32),
+                in_=w1_words[:, :, 2 * GROUP * g : 2 * GROUP * (g + 1)].rearrange("k p n -> p k n").bitcast(I32),
+            )
+
+        def load_x(eng, c):
+            eng.dma_start(
+                out=xw[c][:].bitcast(I32),
+                in_=x_words.rearrange("k p n t -> p k (n t)")[:, :, PACK * CHUNK * c : PACK * CHUNK * (c + 1)].bitcast(I32),
+            )
+
+        def load_w2(g):
+            rows = w2[GROUP * g : GROUP * (g + 1), :].rearrange("(a t b) n -> b a t n", t=PACK, b=4)
+            for b in range(4):
+                nc.sync.dma_start(out=w2_raw[g][b:P:4, :, :], in_=rows[b])
+
+        load_scale_rows(w1s_raw, w1_scales, 0)
+        load_scale_rows(w1s_raw, w1_scales, 1)
+        load_w1(nc.scalar, 0)
+        load_x(nc.scalar, 0)
+        load_scale_rows(w1s_raw, w1_scales, 2)
+        load_scale_rows(w1s_raw, w1_scales, 3)
+        for q in range(QUADS):
+            load_scale_rows(xs, x_scales, q)
+        load_w1(nc.sync, 1)
+        load_w1(nc.sync, 2)
+        load_w2(0)
+        load_w2(1)
+        load_x(nc.sync, 1)
+        load_w2(2)
+        load_x(nc.sync, 2)
+
+        b1_rows = kept([P, F_GROUPS * P], BF16, "b1_rows")
+        nc.gpsimd.memset(b1_rows[:], 0.0)
+        nc.gpsimd.dma_start(
+            out=b1_rows[0:PACK, :].rearrange("t (a b) -> t a b", b=4),
+            in_=b1.rearrange("(a t b) -> t a b", t=PACK, b=4),
+        )
+        ident = kept([P, P], F32, "ident")
+        make_identity(nc, ident[:])
+        cols = []
+        for name, vec in (("b2c", b2), ("basec", baseline), ("vwc", value_w)):
+            col = kept([P, N_GROUPS, PACK], BF16, name)
+            nc.gpsimd.dma_start(out=col[:], in_=vec.rearrange("(g p t) -> p g t", p=P, t=PACK))
+            cols.append(col)
+        b2_col, base_col, vw_col = cols
+
+        ident_bf = kept([P, P], BF16, "ident_bf")
+        nc.scalar.activation(out=ident_bf[:], in_=ident[:], func=ACT.Relu)
+        b1_ps = psum.tile([P, F_GROUPS, P], BF16, name="b1_ps", tag="bank")
+        for g in range(F_GROUPS):
+            nc.tensor.transpose(b1_ps[:, g, :], b1_rows[:, P * g : P * (g + 1)], ident_bf[:])
+        b1_col = kept([P, F_GROUPS, PACK], F32, "b1_col")
+        nc.scalar.copy(out=b1_col[:], in_=b1_ps[:, :, 0:PACK])
+
+        w1w = [kept([P, K_PASSES, PACK, 2 * P], U8, "w1w%d" % g) for g in range(F_GROUPS)]
+        w1s = [kept([P, K_PASSES, PACK, P], U8, "w1s%d" % g) for g in range(F_GROUPS)]
+        for g in range(F_GROUPS):
+            nc.vector.tensor_copy(
+                out=w1s[g][:].bitcast(I32),
+                in_=w1s_raw[:, :, GROUP * g : GROUP * (g + 1)].bitcast(I32).rearrange("p k (a t) -> p k t a", t=PACK),
+            )
+            nc.vector.tensor_copy(
+                out=w1w[g][:].bitcast(I32).rearrange("p k t (a w) -> p k t a w", w=2),
+                in_=w1_raw[g][:].bitcast(I32).rearrange("p k (a t w) -> p k t a w", t=PACK, w=2),
+            )
+
+        h_raw = {}
+        for c in range(CHUNKS):
+            for g in range(F_GROUPS):
+                h_raw[c, g] = kept([P, PACK, CHUNK], BF16, "h_raw%d_%d" % (c, g))
+                for t in range(PACK):
+                    bank = psum.tile([P, CHUNK], F32, name="bank", tag="bank")
+                    for k in range(K_PASSES):
+                        nc.tensor.matmul_mx(
+                            out=bank[:],
+                            lhsT=w1w[g][:, k, t, :].bitcast(FP4X4),
+                            lhsT_scale=w1s[g][:, k, t, :],
+                            rhs=xw[c][:, k, :].bitcast(FP8X4),
+                            rhs_scale=xs[:, k, CHUNK * c : CHUNK * (c + 1)],
+                            start=(k == 0),
+                            stop=(k == K_PASSES - 1),
+                        )
+                    nc.scalar.activation(
+                        out=h_raw[c, g][:, t, :], in_=bank[:], func=ACT.Relu, bias=b1_col[:, g, t : t + 1]
+                    )
+
+        def interleave(src, pattern, **sizes):
+            grouped = work.tile([P, PACK * CHUNK], BF16, name="grouped", align_bytes=64)
+            nc.vector.tensor_copy(out=grouped[:].rearrange(pattern, **sizes), in_=src)
+            return grouped
+
+        def interleave_slots(src):
+            return interleave(
+                src[:].rearrange("p t (c i) -> p c t i", i=4), "p (c i t) -> p c t i", i=4, t=PACK
+            )
+
+        def interleave_w2(g, j):
+            src = w2_raw[g][:, :, GROUP * j : GROUP * (j + 1)].rearrange("p s (c i t) -> p t c s i", i=2, t=PACK)
+            return interleave(src, "p (t c i s) -> p t c s i", t=PACK, i=2, s=PACK)
+
+        def quantize(grouped, codes, scales):
+            nc.vector.quantize_mx(out=codes.bitcast(FP8X4), scales=scales, in_=grouped[:])
+
+        codes = {}
+        scales = {}
+
+        def start_unit(key):
+            codes[key] = kept([P, CHUNK], U32, "codes_%s%d_%d" % key)
+            scales[key] = kept([P, CHUNK], U8, "scales_%s%d_%d" % key)
+            if key[0] == "w":
+                return interleave_w2(key[1], key[2])
+            return interleave_slots(h_raw[key[1], key[2]])
+
+        def finish_unit(key, grouped):
+            quantize(grouped, codes[key][:], scales[key][:])
+
+        order = [("w", 0, 0), ("w", 0, 1), ("h", 0, 0), ("w", 1, 0), ("h", 0, 1), ("w", 2, 0), ("h", 0, 2),
+                 ("w", 1, 1), ("w", 2, 1), ("h", 1, 0), ("h", 1, 1), ("h", 1, 2)]
+        pending = None
+        for key in order:
+            grouped = start_unit(key)
+            if pending is not None:
+                finish_unit(*pending)
+            pending = (key, grouped)
+        finish_unit(*pending)
+
+        y_scales = kept([P, M], U8, "y_scales")
+        units = [(c, j) for c in range(CHUNKS) for j in range(N_GROUPS)]
+        y = {}
+
+        def second(u, t):
+            c, j = units[u]
+            bank = psum.tile([P, CHUNK], F32, name="bank", tag="bank")
+            for g in range(F_GROUPS):
+                nc.tensor.matmul_mx(
+                    out=bank[:],
+                    lhsT=codes["w", g, j][:, P * t : P * (t + 1)].bitcast(FP8X4),
+                    lhsT_scale=scales["w", g, j][:, P * t : P * (t + 1)],
+                    rhs=codes["h", c, g][:].bitcast(FP8X4),
+                    rhs_scale=scales["h", c, g][:],
+                    start=(g == 0),
+                    stop=(g == F_GROUPS - 1),
+                )
+            nc.scalar.activation(out=y[u][:, t, :], in_=bank[:], func=ACT.Relu, bias=b2_col[:, j, t : t + 1])
+
+        def affine(u, t):
+            j = units[u][1]
+            nc.vector.tensor_scalar(
+                out=y[u][:, t, :], in0=y[u][:, t, :],
+                scalar1=base_col[:, j, t : t + 1], scalar2=vw_col[:, j, t : t + 1],
+                op0=ALU.subtract, op1=ALU.mult,
+            )
+
+        def turn(u):
+            c, j = units[u]
+            for i in range(CHUNK // P):
+                bank = psum.tile([P, PACK, P], F32, name="bank", tag="bank")
+                for t in range(PACK):
+                    nc.tensor.transpose(bank[:, t, :], y[u][:, t, P * i : P * (i + 1)], ident[:])
+                rows = work.tile([P, GROUP], F32, name="rows", bufs=6)
+                nc.scalar.copy(
+                    out=rows[:].rearrange("m (p t) -> m p t", t=PACK), in_=bank[:].rearrange("m t p -> m p t")
+                )
+                m0 = CHUNK * c + P * i
+                nc.sync.dma_start(out=out_0[m0 : m0 + P, GROUP * j : GROUP * (j + 1)], in_=rows[:])
+
+        def planes(u, grouped):
+            c, j = units[u]
+            y_codes = work.tile([P, CHUNK], U32, name="y_codes", align_bytes=64)
+            quantize(grouped, y_codes[:], y_scales[PACK * j : P, CHUNK * c : CHUNK * (c + 1)])
+            nc.sync.dma_start(
+                out=out_1[j].rearrange("p m t -> p (m t)")[:, PACK * CHUNK * c : PACK * CHUNK * (c + 1)].bitcast(I32),
+                in_=y_codes[:].bitcast(I32),
+            )
+
+        def store_scales(m0, m1):
+            for q in range(QUADS):
+                nc.sync.dma_start(
+                    out=out_2[:, 4 * q : 4 * q + 4, m0:m1].bitcast(I32),
+                    in_=y_scales[32 * q : 32 * q + 4 * N_GROUPS, m0:m1].bitcast(I32),
+                )
+
+        last = len(units) - 1
+        for u in range(len(units)):
+            y[u] = work.tile([P, PACK, CHUNK], F32, name="y", align_bytes=64)
+            second(u, 0)
+            affine(u, 0)
+            if u > 0:
+                y_grouped = interleave_slots(y[u - 1])
+            second(u, 1)
+            affine(u, 1)
+            if u < F_GROUPS:
+                key = ("h", CHUNKS - 1, u)
+                h_grouped = start_unit(key)
+            if u > 0:
+                turn(u - 1)
+                planes(u - 1, y_grouped)
+            if u == last - 1:
+                store_scales(0, CHUNK * (CHUNKS - 1))
+            second(u, 2)
+            affine(u, 2)
+            if u < F_GROUPS:
+                finish_unit(key, h_grouped)
+            second(u, 3)
+            affine(u, 3)
+        y_grouped = interleave_slots(y[last])
+        planes(last, y_grouped)
+        store_scales(CHUNK * (CHUNKS - 1), M)
+        turn(last)

@@ -42,11 +42,13 @@ def tile_critic_value_contributions_h2_kernel(
 
         w1s_raw = kept([P, K_PASSES, F], U8, "w1s_raw")
         xs = kept([P, K_PASSES, M], U8, "xs")
+        b1_rows = kept([P, GROUP], BF16, "b1_rows")
+        nc.vector.memset(b1_rows[:], 0.0)
         nc.vector.memset(w1s_raw[:].bitcast(I32), 0)
         nc.vector.memset(xs[:].bitcast(I32), 0)
 
-        def load_scale_rows(plane, rows, q):
-            nc.sync.dma_start(
+        def load_scale_rows(eng, plane, rows, q):
+            eng.dma_start(
                 out=plane[32 * q : 32 * q + 4, :, :].bitcast(I32),
                 in_=rows[:, 4 * q : 4 * q + 4, :].rearrange("k r n -> r k n").bitcast(I32),
             )
@@ -72,48 +74,46 @@ def tile_critic_value_contributions_h2_kernel(
             for b in range(4):
                 nc.sync.dma_start(out=w2_raw[g][b:P:4, :, :], in_=rows[b])
 
-        load_scale_rows(w1s_raw, w1_scales, 0)
-        load_scale_rows(w1s_raw, w1_scales, 1)
+        ident = kept([P, P], F32, "ident")
+        make_identity(nc, ident[:])
+        nc.sync.dma_start(out=b1_rows[0:F_GROUPS, :], in_=b1.rearrange("(g f) -> g f", g=F_GROUPS))
         load_w1(nc.scalar, 0)
         load_x(nc.scalar, 0)
-        load_scale_rows(w1s_raw, w1_scales, 2)
-        load_scale_rows(w1s_raw, w1_scales, 3)
         for q in range(QUADS):
-            load_scale_rows(xs, x_scales, q)
+            load_scale_rows(nc.sync, w1s_raw, w1_scales, q)
+        for q in range(QUADS):
+            load_scale_rows(nc.sync if q < 2 else nc.gpsimd, xs, x_scales, q)
         load_w1(nc.sync, 1)
-        load_w1(nc.sync, 2)
         load_w2(0)
+        load_w1(nc.sync, 2)
         load_w2(1)
         load_x(nc.sync, 1)
         load_w2(2)
         load_x(nc.sync, 2)
-
-        b1_rows = kept([P, F_GROUPS * P], BF16, "b1_rows")
-        nc.gpsimd.memset(b1_rows[:], 0.0)
-        nc.gpsimd.dma_start(
-            out=b1_rows[0:PACK, :].rearrange("t (a b) -> t a b", b=4),
-            in_=b1.rearrange("(a t b) -> t a b", t=PACK, b=4),
-        )
-        ident = kept([P, P], F32, "ident")
-        make_identity(nc, ident[:])
         cols = []
         for name, vec in (("b2c", b2), ("basec", baseline), ("vwc", value_w)):
             col = kept([P, N_GROUPS, PACK], BF16, name)
-            nc.gpsimd.dma_start(out=col[:], in_=vec.rearrange("(g p t) -> p g t", p=P, t=PACK))
+            nc.sync.dma_start(out=col[:], in_=vec.rearrange("(g p t) -> p g t", p=P, t=PACK))
             cols.append(col)
         b2_col, base_col, vw_col = cols
 
         ident_bf = kept([P, P], BF16, "ident_bf")
         nc.scalar.activation(out=ident_bf[:], in_=ident[:], func=ACT.Relu)
-        b1_ps = psum.tile([P, F_GROUPS, P], BF16, name="b1_ps", tag="bank")
-        for g in range(F_GROUPS):
-            nc.tensor.transpose(b1_ps[:, g, :], b1_rows[:, P * g : P * (g + 1)], ident_bf[:])
-        b1_col = kept([P, F_GROUPS, PACK], F32, "b1_col")
-        nc.scalar.copy(out=b1_col[:], in_=b1_ps[:, :, 0:PACK])
+        b1_slots = kept([P, PACK, P], BF16, "b1_slots")
+        nc.vector.tensor_copy(
+            out=b1_slots[:].rearrange("g t (a b) -> g t a b", b=4),
+            in_=b1_rows[:].rearrange("g (a t b) -> g t a b", t=PACK, b=4),
+        )
+        b1_ps = psum.tile([P, PACK, P], BF16, name="b1_ps", tag="bank")
+        for t in range(PACK):
+            nc.tensor.transpose(b1_ps[:, t, :], b1_slots[:, t, :], ident_bf[:])
+        b1_col = kept([P, PACK, F_GROUPS], F32, "b1_col")
+        nc.scalar.copy(out=b1_col[:], in_=b1_ps[:, :, 0:F_GROUPS])
 
         w1w = [kept([P, K_PASSES, PACK, 2 * P], U8, "w1w%d" % g) for g in range(F_GROUPS)]
         w1s = [kept([P, K_PASSES, PACK, P], U8, "w1s%d" % g) for g in range(F_GROUPS)]
-        for g in range(F_GROUPS):
+
+        def sort_w1(g):
             nc.vector.tensor_copy(
                 out=w1s[g][:].bitcast(I32),
                 in_=w1s_raw[:, :, GROUP * g : GROUP * (g + 1)].bitcast(I32).rearrange("p k (a t) -> p k t a", t=PACK),
@@ -123,7 +123,86 @@ def tile_critic_value_contributions_h2_kernel(
                 in_=w1_raw[g][:].bitcast(I32).rearrange("p k (a t w) -> p k t a w", t=PACK, w=2),
             )
 
+        def interleave(src, width, pattern, **sizes):
+            grouped = work.tile([P, PACK * width], BF16, name="grouped", align_bytes=64)
+            nc.vector.tensor_copy(out=grouped[:].rearrange(pattern, **sizes), in_=src)
+            return grouped
+
+        def interleave_slots(src):
+            return interleave(
+                src[:].rearrange("p t (c i) -> p c t i", i=4), src.shape[2], "p (c i t) -> p c t i", i=4, t=PACK
+            )
+
+        def interleave_w2(g, j):
+            src = w2_raw[g][:, :, GROUP * j : GROUP * (j + 1)].rearrange("p s (c i t) -> p t c s i", i=2, t=PACK)
+            return interleave(src, GROUP, "p (t c i s) -> p t c s i", t=PACK, i=2, s=PACK)
+
+        def quantize(grouped, words, plane):
+            nc.vector.quantize_mx(out=words.bitcast(FP8X4), scales=plane, in_=grouped[:])
+
+        codes = {}
+        scales = {}
         h_raw = {}
+        y = {}
+        grouped_of = {}
+        unstored = []
+        finished = set()
+        y_scales = kept([P, M], U8, "y_scales")
+        half = CHUNK // 2
+        units = [(j, CHUNK * c, CHUNK) for c in range(CHUNKS) for j in range(N_GROUPS)]
+        j_last, m_last = units[-1][0:2]
+        units = units[:-1] + [(j_last, m_last, half), (j_last, m_last + half, half)]
+
+        def step_interleave(key):
+            if key[0] == "w":
+                grouped_of[key] = interleave_w2(key[1], key[2])
+            elif key[0] == "h":
+                grouped_of[key] = interleave_slots(h_raw[key[1], key[2]])
+            else:
+                grouped_of[key] = interleave_slots(y[key[1]])
+
+        def step_quantize(key):
+            if key[0] == "y":
+                j, m0, width = units[key[1]]
+                y_codes = work.tile([P, width], U32, name="y_codes", align_bytes=64)
+                quantize(grouped_of[key], y_codes[:], y_scales[PACK * j : P, m0 : m0 + width])
+                unstored.append((j, m0, width, y_codes))
+            else:
+                codes[key] = kept([P, CHUNK], U32, "codes_%s%d_%d" % key)
+                scales[key] = kept([P, CHUNK], U8, "scales_%s%d_%d" % key)
+                quantize(grouped_of[key], codes[key][:], scales[key][:])
+
+        def store_codes():
+            for j, m0, width, y_codes in unstored:
+                nc.sync.dma_start(
+                    out=out_1[j].rearrange("p m t -> p (m t)")[:, PACK * m0 : PACK * (m0 + width)].bitcast(I32),
+                    in_=y_codes[:].bitcast(I32),
+                )
+            unstored.clear()
+
+        def staggered(keys):
+            steps = [(step_interleave, keys[0])]
+            for before, key in zip(keys, keys[1:]):
+                steps.extend([(step_interleave, key), (step_quantize, before)])
+            return steps + [(step_quantize, keys[-1])]
+
+        steps = staggered(
+            [("w", 0, 0), ("w", 0, 1), ("h", 0, 0), ("w", 1, 0), ("h", 0, 1), ("w", 2, 0), ("h", 0, 2),
+             ("w", 1, 1), ("w", 2, 1), ("h", 1, 0), ("h", 1, 1), ("h", 1, 2),
+             ("h", 2, 0), ("h", 2, 1), ("h", 2, 2), ("y", 0, 0), ("y", 1, 0), ("y", 2, 0), ("y", 3, 0), ("y", 4, 0), ("y", 5, 0), ("y", 6, 0)]
+        )
+
+        def run_steps(count):
+            for fn, key in steps[:count]:
+                if key[0] == "y" and key[1] not in finished:
+                    break
+                fn(key)
+                steps.remove((fn, key))
+
+        sort_w1(0)
+        sort_w1(1)
+        run_steps(1)
+        sort_w1(2)
         for c in range(CHUNKS):
             for g in range(F_GROUPS):
                 h_raw[c, g] = kept([P, PACK, CHUNK], BF16, "h_raw%d_%d" % (c, g))
@@ -140,70 +219,25 @@ def tile_critic_value_contributions_h2_kernel(
                             stop=(k == K_PASSES - 1),
                         )
                     nc.scalar.activation(
-                        out=h_raw[c, g][:, t, :], in_=bank[:], func=ACT.Relu, bias=b1_col[:, g, t : t + 1]
+                        out=h_raw[c, g][:, t, :], in_=bank[:], func=ACT.Relu, bias=b1_col[:, t, g : g + 1]
                     )
-
-        def interleave(src, pattern, **sizes):
-            grouped = work.tile([P, PACK * CHUNK], BF16, name="grouped", align_bytes=64)
-            nc.vector.tensor_copy(out=grouped[:].rearrange(pattern, **sizes), in_=src)
-            return grouped
-
-        def interleave_slots(src):
-            return interleave(
-                src[:].rearrange("p t (c i) -> p c t i", i=4), "p (c i t) -> p c t i", i=4, t=PACK
-            )
-
-        def interleave_w2(g, j):
-            src = w2_raw[g][:, :, GROUP * j : GROUP * (j + 1)].rearrange("p s (c i t) -> p t c s i", i=2, t=PACK)
-            return interleave(src, "p (t c i s) -> p t c s i", t=PACK, i=2, s=PACK)
-
-        def quantize(grouped, codes, scales):
-            nc.vector.quantize_mx(out=codes.bitcast(FP8X4), scales=scales, in_=grouped[:])
-
-        codes = {}
-        scales = {}
-
-        def start_unit(key):
-            codes[key] = kept([P, CHUNK], U32, "codes_%s%d_%d" % key)
-            scales[key] = kept([P, CHUNK], U8, "scales_%s%d_%d" % key)
-            if key[0] == "w":
-                return interleave_w2(key[1], key[2])
-            return interleave_slots(h_raw[key[1], key[2]])
-
-        def finish_unit(key, grouped):
-            quantize(grouped, codes[key][:], scales[key][:])
-
-        order = [("w", 0, 0), ("w", 0, 1), ("h", 0, 0), ("w", 1, 0), ("h", 0, 1), ("w", 2, 0), ("h", 0, 2),
-                 ("w", 1, 1), ("w", 2, 1), ("h", 1, 0), ("h", 1, 1), ("h", 1, 2)]
-        pending = None
-        for key in order:
-            grouped = start_unit(key)
-            if pending is not None:
-                finish_unit(*pending)
-            pending = (key, grouped)
-        finish_unit(*pending)
-
-        y_scales = kept([P, M], U8, "y_scales")
-        units = [(c, j) for c in range(CHUNKS) for j in range(N_GROUPS)]
-        y = {}
+        run_steps(20)
 
         def second(u, t):
-            c, j = units[u]
-            bank = psum.tile([P, CHUNK], F32, name="bank", tag="bank")
+            j, m0, width = units[u]
+            c, lo = divmod(m0, CHUNK)
+            bank = psum.tile([P, width], F32, name="bank", tag="bank")
             for g in range(F_GROUPS):
                 nc.tensor.matmul_mx(
                     out=bank[:],
                     lhsT=codes["w", g, j][:, P * t : P * (t + 1)].bitcast(FP8X4),
                     lhsT_scale=scales["w", g, j][:, P * t : P * (t + 1)],
-                    rhs=codes["h", c, g][:].bitcast(FP8X4),
-                    rhs_scale=scales["h", c, g][:],
+                    rhs=codes["h", c, g][:, lo : lo + width].bitcast(FP8X4),
+                    rhs_scale=scales["h", c, g][:, lo : lo + width],
                     start=(g == 0),
                     stop=(g == F_GROUPS - 1),
                 )
             nc.scalar.activation(out=y[u][:, t, :], in_=bank[:], func=ACT.Relu, bias=b2_col[:, j, t : t + 1])
-
-        def affine(u, t):
-            j = units[u][1]
             nc.vector.tensor_scalar(
                 out=y[u][:, t, :], in0=y[u][:, t, :],
                 scalar1=base_col[:, j, t : t + 1], scalar2=vw_col[:, j, t : t + 1],
@@ -211,8 +245,8 @@ def tile_critic_value_contributions_h2_kernel(
             )
 
         def turn(u):
-            c, j = units[u]
-            for i in range(CHUNK // P):
+            j, m0, width = units[u]
+            for i in range(width // P):
                 bank = psum.tile([P, PACK, P], F32, name="bank", tag="bank")
                 for t in range(PACK):
                     nc.tensor.transpose(bank[:, t, :], y[u][:, t, P * i : P * (i + 1)], ident[:])
@@ -220,17 +254,9 @@ def tile_critic_value_contributions_h2_kernel(
                 nc.scalar.copy(
                     out=rows[:].rearrange("m (p t) -> m p t", t=PACK), in_=bank[:].rearrange("m t p -> m p t")
                 )
-                m0 = CHUNK * c + P * i
-                nc.sync.dma_start(out=out_0[m0 : m0 + P, GROUP * j : GROUP * (j + 1)], in_=rows[:])
-
-        def planes(u, grouped):
-            c, j = units[u]
-            y_codes = work.tile([P, CHUNK], U32, name="y_codes", align_bytes=64)
-            quantize(grouped, y_codes[:], y_scales[PACK * j : P, CHUNK * c : CHUNK * (c + 1)])
-            nc.sync.dma_start(
-                out=out_1[j].rearrange("p m t -> p (m t)")[:, PACK * CHUNK * c : PACK * CHUNK * (c + 1)].bitcast(I32),
-                in_=y_codes[:].bitcast(I32),
-            )
+                nc.sync.dma_start(
+                    out=out_0[m0 + P * i : m0 + P * (i + 1), GROUP * j : GROUP * (j + 1)], in_=rows[:]
+                )
 
         def store_scales(m0, m1):
             for q in range(QUADS):
@@ -239,30 +265,20 @@ def tile_critic_value_contributions_h2_kernel(
                     in_=y_scales[32 * q : 32 * q + 4 * N_GROUPS, m0:m1].bitcast(I32),
                 )
 
-        last = len(units) - 1
+        PER_UNIT = [4, 4, 4, 4, 4, 4, 4]
         for u in range(len(units)):
-            y[u] = work.tile([P, PACK, CHUNK], F32, name="y", align_bytes=64)
-            second(u, 0)
-            affine(u, 0)
-            if u > 0:
-                y_grouped = interleave_slots(y[u - 1])
-            second(u, 1)
-            affine(u, 1)
-            if u < F_GROUPS:
-                key = ("h", CHUNKS - 1, u)
-                h_grouped = start_unit(key)
-            if u > 0:
-                turn(u - 1)
-                planes(u - 1, y_grouped)
-            if u == last - 1:
-                store_scales(0, CHUNK * (CHUNKS - 1))
-            second(u, 2)
-            affine(u, 2)
-            if u < F_GROUPS:
-                finish_unit(key, h_grouped)
-            second(u, 3)
-            affine(u, 3)
-        y_grouped = interleave_slots(y[last])
-        planes(last, y_grouped)
-        store_scales(CHUNK * (CHUNKS - 1), M)
-        turn(last)
+            width = units[u][2]
+            y[u] = work.tile([P, PACK, width], F32, name="y", bufs=6, align_bytes=64)
+            for t in range(PACK):
+                second(u, t)
+                if t == PACK - 1:
+                    finished.add(u)
+                if t < PER_UNIT[u]:
+                    run_steps(1)
+                if u > 0 and t == PACK - 1:
+                    turn(u - 1)
+                    store_codes()
+        turn(len(units) - 1)
+        run_steps(len(steps))
+        store_codes()
+        store_scales(0, M)

@@ -41,21 +41,24 @@ def tile_critic_value_contributions_h2_kernel(
             return keep.tile(shape, dtype, name=name, align_bytes=64)
 
         w1s_raw = kept([P, K_PASSES, F], U8, "w1s_raw")
-        xs = kept([P, K_PASSES, M], U8, "xs")
+        xs_first = kept([P, K_PASSES, CHUNK], U8, "xs_first")
+        xs_rest = kept([P, K_PASSES, M - CHUNK], U8, "xs_rest")
         b1_rows = kept([P, GROUP], BF16, "b1_rows")
         nc.vector.memset(b1_rows[:], 0.0)
         nc.vector.memset(w1s_raw[:].bitcast(I32), 0)
-        nc.vector.memset(xs[:].bitcast(I32), 0)
+        nc.vector.memset(xs_first[:].bitcast(I32), 0)
+        nc.vector.memset(xs_rest[:].bitcast(I32), 0)
+        xs = [xs_first[:]] + [xs_rest[:, :, CHUNK * c : CHUNK * (c + 1)] for c in range(CHUNKS - 1)]
 
-        def load_scale_rows(eng, plane, rows, q):
-            eng.dma_start(
+        def load_scale_rows(plane, rows, q, lo, hi):
+            nc.sync.dma_start(
                 out=plane[32 * q : 32 * q + 4, :, :].bitcast(I32),
-                in_=rows[:, 4 * q : 4 * q + 4, :].rearrange("k r n -> r k n").bitcast(I32),
+                in_=rows[:, 4 * q : 4 * q + 4, lo:hi].rearrange("k r n -> r k n").bitcast(I32),
             )
 
         w1_raw = [kept([P, K_PASSES, 2 * GROUP], U8, "w1_raw%d" % g) for g in range(F_GROUPS)]
         xw = [kept([P, K_PASSES, CHUNK], U32, "xw%d" % c) for c in range(CHUNKS)]
-        w2_raw = [kept([P, PACK, N], BF16, "w2_raw%d" % g) for g in range(F_GROUPS)]
+        w2_raw = {(g, j): kept([P, PACK, GROUP], BF16, "w2_raw%d_%d" % (g, j)) for g in range(F_GROUPS) for j in range(N_GROUPS)}
 
         def load_w1(eng, g):
             eng.dma_start(
@@ -69,26 +72,42 @@ def tile_critic_value_contributions_h2_kernel(
                 in_=x_words.rearrange("k p n t -> p k (n t)")[:, :, PACK * CHUNK * c : PACK * CHUNK * (c + 1)].bitcast(I32),
             )
 
-        def load_w2(g):
-            rows = w2[GROUP * g : GROUP * (g + 1), :].rearrange("(a t b) n -> b a t n", t=PACK, b=4)
+        def load_w2(g, j):
+            rows = w2[GROUP * g : GROUP * (g + 1), GROUP * j : GROUP * (j + 1)].rearrange("(a t b) n -> b a t n", t=PACK, b=4)
             for b in range(4):
-                nc.sync.dma_start(out=w2_raw[g][b:P:4, :, :], in_=rows[b])
+                nc.sync.dma_start(out=w2_raw[g, j][b:P:4, :, :], in_=rows[b])
+
+        def load_b1():
+            nc.scalar.dma_start(out=b1_rows[0:F_GROUPS, :], in_=b1.rearrange("(g f) -> g f", g=F_GROUPS))
 
         ident = kept([P, P], F32, "ident")
         make_identity(nc, ident[:])
-        nc.sync.dma_start(out=b1_rows[0:F_GROUPS, :], in_=b1.rearrange("(g f) -> g f", g=F_GROUPS))
+        ident_bf = kept([P, P], BF16, "ident_bf")
         load_w1(nc.scalar, 0)
-        load_x(nc.scalar, 0)
-        for q in range(QUADS):
-            load_scale_rows(nc.sync, w1s_raw, w1_scales, q)
-        for q in range(QUADS):
-            load_scale_rows(nc.sync if q < 2 else nc.gpsimd, xs, x_scales, q)
+        load_b1()
+        nc.scalar.activation(out=ident_bf[:], in_=ident[:], func=ACT.Relu)
+        load_scale_rows(w1s_raw, w1_scales, 0, 0, 1536)
+        load_scale_rows(w1s_raw, w1_scales, 1, 0, 1536)
+        load_x(nc.sync, 0)
+        load_scale_rows(w1s_raw, w1_scales, 2, 0, 1536)
+        load_scale_rows(w1s_raw, w1_scales, 3, 0, 1536)
+        load_scale_rows(xs_first, x_scales, 0, 0, 512)
+        load_scale_rows(xs_first, x_scales, 1, 0, 512)
+        load_scale_rows(xs_first, x_scales, 2, 0, 512)
+        load_scale_rows(xs_first, x_scales, 3, 0, 512)
         load_w1(nc.sync, 1)
-        load_w2(0)
+        load_w2(0, 0)
         load_w1(nc.sync, 2)
-        load_w2(1)
+        load_w2(1, 0)
+        load_w2(2, 0)
+        load_scale_rows(xs_rest, x_scales, 0, 512, 1536)
+        load_scale_rows(xs_rest, x_scales, 1, 512, 1536)
+        load_scale_rows(xs_rest, x_scales, 2, 512, 1536)
+        load_scale_rows(xs_rest, x_scales, 3, 512, 1536)
         load_x(nc.sync, 1)
-        load_w2(2)
+        load_w2(0, 1)
+        load_w2(1, 1)
+        load_w2(2, 1)
         load_x(nc.sync, 2)
         cols = []
         for name, vec in (("b2c", b2), ("basec", baseline), ("vwc", value_w)):
@@ -96,19 +115,6 @@ def tile_critic_value_contributions_h2_kernel(
             nc.sync.dma_start(out=col[:], in_=vec.rearrange("(g p t) -> p g t", p=P, t=PACK))
             cols.append(col)
         b2_col, base_col, vw_col = cols
-
-        ident_bf = kept([P, P], BF16, "ident_bf")
-        nc.scalar.activation(out=ident_bf[:], in_=ident[:], func=ACT.Relu)
-        b1_slots = kept([P, PACK, P], BF16, "b1_slots")
-        nc.vector.tensor_copy(
-            out=b1_slots[:].rearrange("g t (a b) -> g t a b", b=4),
-            in_=b1_rows[:].rearrange("g (a t b) -> g t a b", t=PACK, b=4),
-        )
-        b1_ps = psum.tile([P, PACK, P], BF16, name="b1_ps", tag="bank")
-        for t in range(PACK):
-            nc.tensor.transpose(b1_ps[:, t, :], b1_slots[:, t, :], ident_bf[:])
-        b1_col = kept([P, PACK, F_GROUPS], F32, "b1_col")
-        nc.scalar.copy(out=b1_col[:], in_=b1_ps[:, :, 0:F_GROUPS])
 
         w1w = [kept([P, K_PASSES, PACK, 2 * P], U8, "w1w%d" % g) for g in range(F_GROUPS)]
         w1s = [kept([P, K_PASSES, PACK, P], U8, "w1s%d" % g) for g in range(F_GROUPS)]
@@ -134,7 +140,7 @@ def tile_critic_value_contributions_h2_kernel(
             )
 
         def interleave_w2(g, j):
-            src = w2_raw[g][:, :, GROUP * j : GROUP * (j + 1)].rearrange("p s (c i t) -> p t c s i", i=2, t=PACK)
+            src = w2_raw[g, j][:].rearrange("p s (c i t) -> p t c s i", i=2, t=PACK)
             return interleave(src, GROUP, "p (t c i s) -> p t c s i", t=PACK, i=2, s=PACK)
 
         def quantize(grouped, words, plane):
@@ -178,6 +184,8 @@ def tile_critic_value_contributions_h2_kernel(
                     out=out_1[j].rearrange("p m t -> p (m t)")[:, PACK * m0 : PACK * (m0 + width)].bitcast(I32),
                     in_=y_codes[:].bitcast(I32),
                 )
+                if j == N_GROUPS - 1 and (m0 + width) % CHUNK == 0:
+                    store_scales(m0 + width - CHUNK, m0 + width)
             unstored.clear()
 
         def staggered(keys):
@@ -187,8 +195,7 @@ def tile_critic_value_contributions_h2_kernel(
             return steps + [(step_quantize, keys[-1])]
 
         steps = staggered(
-            [("w", 0, 0), ("w", 0, 1), ("h", 0, 0), ("w", 1, 0), ("h", 0, 1), ("w", 2, 0), ("h", 0, 2),
-             ("w", 1, 1), ("w", 2, 1), ("h", 1, 0), ("h", 1, 1), ("h", 1, 2),
+            [("w", 0, 0), ("w", 1, 0), ("h", 0, 0), ("w", 2, 0), ("h", 0, 1), ("w", 0, 1), ("h", 0, 2), ("w", 1, 1), ("w", 2, 1), ("h", 1, 0), ("h", 1, 1), ("h", 1, 2),
              ("h", 2, 0), ("h", 2, 1), ("h", 2, 2), ("y", 0, 0), ("y", 1, 0), ("y", 2, 0), ("y", 3, 0), ("y", 4, 0), ("y", 5, 0), ("y", 6, 0)]
         )
 
@@ -198,6 +205,17 @@ def tile_critic_value_contributions_h2_kernel(
                     break
                 fn(key)
                 steps.remove((fn, key))
+
+        b1_slots = kept([P, PACK, P], BF16, "b1_slots")
+        nc.vector.tensor_copy(
+            out=b1_slots[:].rearrange("g t (a b) -> g t a b", b=4),
+            in_=b1_rows[:].rearrange("g (a t b) -> g t a b", t=PACK, b=4),
+        )
+        b1_ps = psum.tile([P, PACK, P], BF16, name="b1_ps", tag="bank")
+        for t in range(PACK):
+            nc.tensor.transpose(b1_ps[:, t, :], b1_slots[:, t, :], ident_bf[:])
+        b1_col = kept([P, PACK, F_GROUPS], F32, "b1_col")
+        nc.scalar.copy(out=b1_col[:], in_=b1_ps[:, :, 0:F_GROUPS])
 
         sort_w1(0)
         sort_w1(1)
@@ -214,14 +232,14 @@ def tile_critic_value_contributions_h2_kernel(
                             lhsT=w1w[g][:, k, t, :].bitcast(FP4X4),
                             lhsT_scale=w1s[g][:, k, t, :],
                             rhs=xw[c][:, k, :].bitcast(FP8X4),
-                            rhs_scale=xs[:, k, CHUNK * c : CHUNK * (c + 1)],
+                            rhs_scale=xs[c][:, k, :],
                             start=(k == 0),
                             stop=(k == K_PASSES - 1),
                         )
                     nc.scalar.activation(
                         out=h_raw[c, g][:, t, :], in_=bank[:], func=ACT.Relu, bias=b1_col[:, t, g : g + 1]
                     )
-        run_steps(20)
+        run_steps(19)
 
         def second(u, t):
             j, m0, width = units[u]
@@ -281,4 +299,3 @@ def tile_critic_value_contributions_h2_kernel(
         turn(len(units) - 1)
         run_steps(len(steps))
         store_codes()
-        store_scales(0, M)

@@ -56,14 +56,16 @@ def tile_critic_value_contributions_h2_kernel(
                 in_=rows[:, 4 * q : 4 * q + 4, lo:hi].rearrange("k r n -> r k n").bitcast(I32),
             )
 
-        w1_raw = [kept([P, K_PASSES, 2 * GROUP], U8, "w1_raw%d" % g) for g in range(F_GROUPS)]
+        w1_first = kept([P, K_PASSES, 2 * GROUP], U8, "w1_first")
+        w1_rest = kept([P, K_PASSES, 2 * (F - GROUP)], U8, "w1_rest")
+        w1_raw = [w1_first[:]] + [w1_rest[:, :, 2 * GROUP * g : 2 * GROUP * (g + 1)] for g in range(F_GROUPS - 1)]
         xw = [kept([P, K_PASSES, CHUNK], U32, "xw%d" % c) for c in range(CHUNKS)]
         w2_raw = {(g, j): kept([P, PACK, GROUP], BF16, "w2_raw%d_%d" % (g, j)) for g in range(F_GROUPS) for j in range(N_GROUPS)}
 
-        def load_w1(eng, g):
+        def load_w1(eng, dst, f0, f1):
             eng.dma_start(
-                out=w1_raw[g][:].bitcast(I32),
-                in_=w1_words[:, :, 2 * GROUP * g : 2 * GROUP * (g + 1)].rearrange("k p n -> p k n").bitcast(I32),
+                out=dst[:].bitcast(I32),
+                in_=w1_words[:, :, 2 * f0 : 2 * f1].rearrange("k p n -> p k n").bitcast(I32),
             )
 
         def load_x(eng, c):
@@ -83,27 +85,26 @@ def tile_critic_value_contributions_h2_kernel(
         ident = kept([P, P], F32, "ident")
         make_identity(nc, ident[:])
         ident_bf = kept([P, P], BF16, "ident_bf")
-        load_w1(nc.scalar, 0)
+        load_w1(nc.scalar, w1_first, 0, GROUP)
         load_b1()
         nc.scalar.activation(out=ident_bf[:], in_=ident[:], func=ACT.Relu)
-        load_scale_rows(w1s_raw, w1_scales, 0, 0, 1536)
-        load_scale_rows(w1s_raw, w1_scales, 1, 0, 1536)
+        load_scale_rows(w1s_raw, w1_scales, 0, 0, F)
+        load_scale_rows(w1s_raw, w1_scales, 2, 0, F)
+        load_scale_rows(w1s_raw, w1_scales, 1, 0, F)
+        load_scale_rows(w1s_raw, w1_scales, 3, 0, F)
         load_x(nc.sync, 0)
-        load_scale_rows(w1s_raw, w1_scales, 2, 0, 1536)
-        load_scale_rows(w1s_raw, w1_scales, 3, 0, 1536)
-        load_scale_rows(xs_first, x_scales, 0, 0, 512)
-        load_scale_rows(xs_first, x_scales, 1, 0, 512)
-        load_scale_rows(xs_first, x_scales, 2, 0, 512)
-        load_scale_rows(xs_first, x_scales, 3, 0, 512)
-        load_w1(nc.sync, 1)
+        load_scale_rows(xs_first, x_scales, 0, 0, CHUNK)
+        load_scale_rows(xs_first, x_scales, 2, 0, CHUNK)
+        load_scale_rows(xs_first, x_scales, 1, 0, CHUNK)
+        load_scale_rows(xs_first, x_scales, 3, 0, CHUNK)
+        load_w1(nc.sync, w1_rest, GROUP, F)
         load_w2(0, 0)
-        load_w1(nc.sync, 2)
         load_w2(1, 0)
         load_w2(2, 0)
-        load_scale_rows(xs_rest, x_scales, 0, 512, 1536)
-        load_scale_rows(xs_rest, x_scales, 1, 512, 1536)
-        load_scale_rows(xs_rest, x_scales, 2, 512, 1536)
-        load_scale_rows(xs_rest, x_scales, 3, 512, 1536)
+        load_scale_rows(xs_rest, x_scales, 0, CHUNK, M)
+        load_scale_rows(xs_rest, x_scales, 1, CHUNK, M)
+        load_scale_rows(xs_rest, x_scales, 2, CHUNK, M)
+        load_scale_rows(xs_rest, x_scales, 3, CHUNK, M)
         load_x(nc.sync, 1)
         load_w2(0, 1)
         load_w2(1, 1)
@@ -126,7 +127,7 @@ def tile_critic_value_contributions_h2_kernel(
             )
             nc.vector.tensor_copy(
                 out=w1w[g][:].bitcast(I32).rearrange("p k t (a w) -> p k t a w", w=2),
-                in_=w1_raw[g][:].bitcast(I32).rearrange("p k (a t w) -> p k t a w", t=PACK, w=2),
+                in_=w1_raw[g].bitcast(I32).rearrange("p k (a t w) -> p k t a w", t=PACK, w=2),
             )
 
         def interleave(src, width, pattern, **sizes):
@@ -136,12 +137,12 @@ def tile_critic_value_contributions_h2_kernel(
 
         def interleave_slots(src):
             return interleave(
-                src[:].rearrange("p t (c i) -> p c t i", i=4), src.shape[2], "p (c i t) -> p c t i", i=4, t=PACK
+                src[:].rearrange("p t m -> p m t"), src.shape[2], "p (m t) -> p m t", t=PACK
             )
 
         def interleave_w2(g, j):
-            src = w2_raw[g, j][:].rearrange("p s (c i t) -> p t c s i", i=2, t=PACK)
-            return interleave(src, GROUP, "p (t c i s) -> p t c s i", t=PACK, i=2, s=PACK)
+            src = w2_raw[g, j][:].rearrange("p s (m t) -> p t m s", t=PACK)
+            return interleave(src, GROUP, "p (t m s) -> p t m s", t=PACK, s=PACK)
 
         def quantize(grouped, words, plane):
             nc.vector.quantize_mx(out=words.bitcast(FP8X4), scales=plane, in_=grouped[:])
@@ -156,8 +157,7 @@ def tile_critic_value_contributions_h2_kernel(
         y_scales = kept([P, M], U8, "y_scales")
         half = CHUNK // 2
         units = [(j, CHUNK * c, CHUNK) for c in range(CHUNKS) for j in range(N_GROUPS)]
-        j_last, m_last = units[-1][0:2]
-        units = units[:-1] + [(j_last, m_last, half), (j_last, m_last + half, half)]
+        units = units[:-1] + [(j, m0 + lo, half) for j, m0, width in units[-1:] for lo in (0, half)]
 
         def step_interleave(key):
             if key[0] == "w":
@@ -170,7 +170,7 @@ def tile_critic_value_contributions_h2_kernel(
         def step_quantize(key):
             if key[0] == "y":
                 j, m0, width = units[key[1]]
-                y_codes = work.tile([P, width], U32, name="y_codes", align_bytes=64)
+                y_codes = work.tile([P, width], U32, name="y_codes", bufs=4, align_bytes=64)
                 quantize(grouped_of[key], y_codes[:], y_scales[PACK * j : P, m0 : m0 + width])
                 unstored.append((j, m0, width, y_codes))
             else:
@@ -178,15 +178,15 @@ def tile_critic_value_contributions_h2_kernel(
                 scales[key] = kept([P, CHUNK], U8, "scales_%s%d_%d" % key)
                 quantize(grouped_of[key], codes[key][:], scales[key][:])
 
-        def store_codes():
-            for j, m0, width, y_codes in unstored:
+        def store_codes(count):
+            for j, m0, width, y_codes in unstored[:count]:
                 nc.sync.dma_start(
                     out=out_1[j].rearrange("p m t -> p (m t)")[:, PACK * m0 : PACK * (m0 + width)].bitcast(I32),
                     in_=y_codes[:].bitcast(I32),
                 )
                 if j == N_GROUPS - 1 and (m0 + width) % CHUNK == 0:
                     store_scales(m0 + width - CHUNK, m0 + width)
-            unstored.clear()
+            unstored[:count] = []
 
         def staggered(keys):
             steps = [(step_interleave, keys[0])]
@@ -195,9 +195,12 @@ def tile_critic_value_contributions_h2_kernel(
             return steps + [(step_quantize, keys[-1])]
 
         steps = staggered(
-            [("w", 0, 0), ("w", 1, 0), ("h", 0, 0), ("w", 2, 0), ("h", 0, 1), ("w", 0, 1), ("h", 0, 2), ("w", 1, 1), ("w", 2, 1), ("h", 1, 0), ("h", 1, 1), ("h", 1, 2),
-             ("h", 2, 0), ("h", 2, 1), ("h", 2, 2), ("y", 0, 0), ("y", 1, 0), ("y", 2, 0), ("y", 3, 0), ("y", 4, 0), ("y", 5, 0), ("y", 6, 0)]
-        )
+            [("w", 0, 0), ("w", 1, 0), ("h", 0, 0), ("w", 2, 0), ("h", 0, 1), ("w", 0, 1), ("h", 0, 2), ("w", 1, 1), ("w", 2, 1), ("h", 1, 0), ("h", 1, 1), ("h", 1, 2), ("h", 2, 0), ("h", 2, 1), ("h", 2, 2)]
+        ) + [
+            (fn, key)
+            for key in [] + [("y", u, 0) for u in range(len(units))]
+            for fn in (step_interleave, step_quantize)
+        ]
 
         def run_steps(count):
             for fn, key in steps[:count]:
@@ -219,7 +222,6 @@ def tile_critic_value_contributions_h2_kernel(
 
         sort_w1(0)
         sort_w1(1)
-        run_steps(1)
         sort_w1(2)
         for c in range(CHUNKS):
             for g in range(F_GROUPS):
@@ -239,7 +241,7 @@ def tile_critic_value_contributions_h2_kernel(
                     nc.scalar.activation(
                         out=h_raw[c, g][:, t, :], in_=bank[:], func=ACT.Relu, bias=b1_col[:, t, g : g + 1]
                     )
-        run_steps(19)
+        run_steps(21)
 
         def second(u, t):
             j, m0, width = units[u]
@@ -262,19 +264,22 @@ def tile_critic_value_contributions_h2_kernel(
                 op0=ALU.subtract, op1=ALU.mult,
             )
 
+        turned = []
+
         def turn(u):
             j, m0, width = units[u]
             for i in range(width // P):
                 bank = psum.tile([P, PACK, P], F32, name="bank", tag="bank")
                 for t in range(PACK):
                     nc.tensor.transpose(bank[:, t, :], y[u][:, t, P * i : P * (i + 1)], ident[:])
+                turned.append((bank, m0 + P * i, j))
+
+        def store_rows(count, copy):
+            for bank, m0, j in turned[:count]:
                 rows = work.tile([P, GROUP], F32, name="rows", bufs=6)
-                nc.scalar.copy(
-                    out=rows[:].rearrange("m (p t) -> m p t", t=PACK), in_=bank[:].rearrange("m t p -> m p t")
-                )
-                nc.sync.dma_start(
-                    out=out_0[m0 + P * i : m0 + P * (i + 1), GROUP * j : GROUP * (j + 1)], in_=rows[:]
-                )
+                copy(out=rows[:].rearrange("m (p t) -> m p t", t=PACK), in_=bank[:].rearrange("m t p -> m p t"))
+                nc.sync.dma_start(out=out_0[m0 : m0 + P, GROUP * j : GROUP * (j + 1)], in_=rows[:])
+            turned[:count] = []
 
         def store_scales(m0, m1):
             for q in range(QUADS):
@@ -283,19 +288,20 @@ def tile_critic_value_contributions_h2_kernel(
                     in_=y_scales[32 * q : 32 * q + 4 * N_GROUPS, m0:m1].bitcast(I32),
                 )
 
-        PER_UNIT = [4, 4, 4, 4, 4, 4, 4]
         for u in range(len(units)):
-            width = units[u][2]
-            y[u] = work.tile([P, PACK, width], F32, name="y", bufs=6, align_bytes=64)
+            y[u] = work.tile([P, PACK, units[u][2]], F32, name="y", bufs=6, align_bytes=64)
             for t in range(PACK):
                 second(u, t)
-                if t == PACK - 1:
-                    finished.add(u)
-                if t < PER_UNIT[u]:
-                    run_steps(1)
-                if u > 0 and t == PACK - 1:
-                    turn(u - 1)
-                    store_codes()
+                if t == 0:
+                    finished.add(u - 1)
+                run_steps(1)
+            if u > 0:
+                turn(u - 1)
+                store_rows(4, nc.scalar.copy)
+                store_codes(max(len(unstored) - 0, 0))
         turn(len(units) - 1)
+        finished.add(len(units) - 1)
+        store_codes(len(unstored))
+        store_rows(2, nc.scalar.copy)
         run_steps(len(steps))
-        store_codes()
+        store_codes(len(unstored))

@@ -17,14 +17,20 @@ ACT = mybir.ActivationFunctionType
 ALU = mybir.AluOpType
 
 P = 128
-PACK = 4
-GROUP = P * PACK
+SLOTS = 4
+GROUP = P * SLOTS
+RUN = 4
 CHUNK = 512
 K_PASSES = K // GROUP
 F_GROUPS = F // GROUP
 N_GROUPS = N // GROUP
 CHUNKS = M // CHUNK
-QUADS = 4
+QUADRANT = 32
+SCALE_ROWS = 4
+QUADRANT_ORDER = (0, 2, 1, 3)
+STEPS_IN_LAYER_1 = 21
+STEPS_BEFORE_CONSTANTS = 12
+SCALAR_SLOTS = (2, 1, 1)
 
 
 def tile_critic_value_contributions_h2_kernel(
@@ -50,114 +56,92 @@ def tile_critic_value_contributions_h2_kernel(
         nc.vector.memset(xs_rest[:].bitcast(I32), 0)
         xs = [xs_first[:]] + [xs_rest[:, :, CHUNK * c : CHUNK * (c + 1)] for c in range(CHUNKS - 1)]
 
-        def load_scale_rows(plane, rows, q, lo, hi):
-            nc.sync.dma_start(
-                out=plane[32 * q : 32 * q + 4, :, :].bitcast(I32),
-                in_=rows[:, 4 * q : 4 * q + 4, lo:hi].rearrange("k r n -> r k n").bitcast(I32),
-            )
-
         w1_first = kept([P, K_PASSES, 2 * GROUP], U8, "w1_first")
         w1_rest = kept([P, K_PASSES, 2 * (F - GROUP)], U8, "w1_rest")
         w1_raw = [w1_first[:]] + [w1_rest[:, :, 2 * GROUP * g : 2 * GROUP * (g + 1)] for g in range(F_GROUPS - 1)]
         xw = [kept([P, K_PASSES, CHUNK], U32, "xw%d" % c) for c in range(CHUNKS)]
-        w2_raw = {(g, j): kept([P, PACK, GROUP], BF16, "w2_raw%d_%d" % (g, j)) for g in range(F_GROUPS) for j in range(N_GROUPS)}
+        w2_raw = {
+            (g, j): kept([P, SLOTS, GROUP], BF16, "w2_raw%d_%d" % (g, j))
+            for g in range(F_GROUPS)
+            for j in range(N_GROUPS)
+        }
 
-        def load_w1(eng, dst, f0, f1):
-            eng.dma_start(
+        def load_scales(plane, rows, lo, hi):
+            for q in QUADRANT_ORDER:
+                nc.sync.dma_start(
+                    out=plane[QUADRANT * q : QUADRANT * q + SCALE_ROWS, :, :].bitcast(I32),
+                    in_=rows[:, SCALE_ROWS * q : SCALE_ROWS * (q + 1), lo:hi].rearrange("k r n -> r k n").bitcast(I32),
+                )
+
+        def load_w1(engine, dst, f0, f1):
+            engine.dma_start(
                 out=dst[:].bitcast(I32),
                 in_=w1_words[:, :, 2 * f0 : 2 * f1].rearrange("k p n -> p k n").bitcast(I32),
             )
 
-        def load_x(eng, c):
-            eng.dma_start(
-                out=xw[c][:].bitcast(I32),
-                in_=x_words.rearrange("k p n t -> p k (n t)")[:, :, PACK * CHUNK * c : PACK * CHUNK * (c + 1)].bitcast(I32),
+        def load_x(c):
+            words = x_words.rearrange("k p n t -> p k (n t)")
+            nc.sync.dma_start(
+                out=xw[c][:].bitcast(I32), in_=words[:, :, SLOTS * CHUNK * c : SLOTS * CHUNK * (c + 1)].bitcast(I32)
             )
 
         def load_w2(g, j):
-            rows = w2[GROUP * g : GROUP * (g + 1), GROUP * j : GROUP * (j + 1)].rearrange("(a t b) n -> b a t n", t=PACK, b=4)
-            for b in range(4):
-                nc.sync.dma_start(out=w2_raw[g, j][b:P:4, :, :], in_=rows[b])
-
-        def load_b1():
-            nc.scalar.dma_start(out=b1_rows[0:F_GROUPS, :], in_=b1.rearrange("(g f) -> g f", g=F_GROUPS))
+            rows = w2[GROUP * g : GROUP * (g + 1), GROUP * j : GROUP * (j + 1)]
+            rows = rows.rearrange("(a t b) n -> b a t n", t=SLOTS, b=RUN)
+            for b in range(RUN):
+                nc.sync.dma_start(out=w2_raw[g, j][b:P:RUN, :, :], in_=rows[b])
 
         ident = kept([P, P], F32, "ident")
         make_identity(nc, ident[:])
         ident_bf = kept([P, P], BF16, "ident_bf")
         load_w1(nc.scalar, w1_first, 0, GROUP)
-        load_b1()
+        nc.scalar.dma_start(out=b1_rows[0:F_GROUPS, :], in_=b1.rearrange("(g f) -> g f", g=F_GROUPS))
         nc.scalar.activation(out=ident_bf[:], in_=ident[:], func=ACT.Relu)
-        load_scale_rows(w1s_raw, w1_scales, 0, 0, F)
-        load_scale_rows(w1s_raw, w1_scales, 2, 0, F)
-        load_scale_rows(w1s_raw, w1_scales, 1, 0, F)
-        load_scale_rows(w1s_raw, w1_scales, 3, 0, F)
-        load_x(nc.sync, 0)
-        load_scale_rows(xs_first, x_scales, 0, 0, CHUNK)
-        load_scale_rows(xs_first, x_scales, 2, 0, CHUNK)
-        load_scale_rows(xs_first, x_scales, 1, 0, CHUNK)
-        load_scale_rows(xs_first, x_scales, 3, 0, CHUNK)
+        load_scales(w1s_raw, w1_scales, 0, F)
+        load_x(0)
+        load_scales(xs_first, x_scales, 0, CHUNK)
         load_w1(nc.sync, w1_rest, GROUP, F)
-        load_w2(0, 0)
-        load_w2(1, 0)
-        load_w2(2, 0)
-        load_scale_rows(xs_rest, x_scales, 0, CHUNK, M)
-        load_scale_rows(xs_rest, x_scales, 1, CHUNK, M)
-        load_scale_rows(xs_rest, x_scales, 2, CHUNK, M)
-        load_scale_rows(xs_rest, x_scales, 3, CHUNK, M)
-        load_x(nc.sync, 1)
-        load_w2(0, 1)
-        load_w2(1, 1)
-        load_w2(2, 1)
-        load_x(nc.sync, 2)
-        cols = []
-        for name, vec in (("b2c", b2), ("basec", baseline), ("vwc", value_w)):
-            col = kept([P, N_GROUPS, PACK], BF16, name)
-            nc.sync.dma_start(out=col[:], in_=vec.rearrange("(g p t) -> p g t", p=P, t=PACK))
-            cols.append(col)
-        b2_col, base_col, vw_col = cols
-
-        w1w = [kept([P, K_PASSES, PACK, 2 * P], U8, "w1w%d" % g) for g in range(F_GROUPS)]
-        w1s = [kept([P, K_PASSES, PACK, P], U8, "w1s%d" % g) for g in range(F_GROUPS)]
-
-        def sort_w1(g):
-            nc.vector.tensor_copy(
-                out=w1s[g][:].bitcast(I32),
-                in_=w1s_raw[:, :, GROUP * g : GROUP * (g + 1)].bitcast(I32).rearrange("p k (a t) -> p k t a", t=PACK),
-            )
-            nc.vector.tensor_copy(
-                out=w1w[g][:].bitcast(I32).rearrange("p k t (a w) -> p k t a w", w=2),
-                in_=w1_raw[g].bitcast(I32).rearrange("p k (a t w) -> p k t a w", t=PACK, w=2),
-            )
-
-        def interleave(src, width, pattern, **sizes):
-            grouped = work.tile([P, PACK * width], BF16, name="grouped", align_bytes=64)
-            nc.vector.tensor_copy(out=grouped[:].rearrange(pattern, **sizes), in_=src)
-            return grouped
-
-        def interleave_slots(src):
-            return interleave(
-                src[:].rearrange("p t m -> p m t"), src.shape[2], "p (m t) -> p m t", t=PACK
-            )
-
-        def interleave_w2(g, j):
-            src = w2_raw[g, j][:].rearrange("p s (m t) -> p t m s", t=PACK)
-            return interleave(src, GROUP, "p (t m s) -> p t m s", t=PACK, s=PACK)
-
-        def quantize(grouped, words, plane):
-            nc.vector.quantize_mx(out=words.bitcast(FP8X4), scales=plane, in_=grouped[:])
+        for g in range(F_GROUPS):
+            load_w2(g, 0)
+        load_scales(xs_rest, x_scales, CHUNK, M)
+        load_x(1)
+        for g in range(F_GROUPS):
+            load_w2(g, 1)
+        load_x(2)
+        unit_cols = []
+        for name, vec in (("b2_col", b2), ("base_col", baseline), ("vw_col", value_w)):
+            col = kept([P, N_GROUPS, SLOTS], BF16, name)
+            nc.sync.dma_start(out=col[:], in_=vec.rearrange("(j p t) -> p j t", p=P, t=SLOTS))
+            unit_cols.append(col)
+        b2_col, base_col, vw_col = unit_cols
 
         codes = {}
         scales = {}
         h_raw = {}
         y = {}
         grouped_of = {}
-        unstored = []
+        unstored_codes = []
         finished = set()
         y_scales = kept([P, M], U8, "y_scales")
         half = CHUNK // 2
-        units = [(j, CHUNK * c, CHUNK) for c in range(CHUNKS) for j in range(N_GROUPS)]
-        units = units[:-1] + [(j, m0 + lo, half) for j, m0, width in units[-1:] for lo in (0, half)]
+        pieces = [(j, CHUNK * c, CHUNK) for c in range(CHUNKS) for j in range(N_GROUPS)]
+        pieces = pieces[:-1] + [(N_GROUPS - 1, M - CHUNK, half), (N_GROUPS - 1, M - half, half)]
+
+        def interleave(src, width, pattern, **sizes):
+            grouped = work.tile([P, SLOTS * width], BF16, name="grouped", align_bytes=64)
+            nc.vector.tensor_copy(out=grouped[:].rearrange(pattern, **sizes), in_=src)
+            return grouped
+
+        def interleave_slots(src):
+            walk = src[:].rearrange("p t (c i) -> p c t i", i=4)
+            return interleave(walk, src.shape[2], "p (c i t) -> p c t i", i=4, t=SLOTS)
+
+        def interleave_w2(g, j):
+            walk = w2_raw[g, j][:].rearrange("p s (c i t) -> p t c s i", i=2, t=SLOTS)
+            return interleave(walk, GROUP, "p (t c i s) -> p t c s i", t=SLOTS, i=2, s=SLOTS)
+
+        def quantize(grouped, words, plane):
+            nc.vector.quantize_mx(out=words.bitcast(FP8X4), scales=plane, in_=grouped[:])
 
         def step_interleave(key):
             if key[0] == "w":
@@ -169,64 +153,62 @@ def tile_critic_value_contributions_h2_kernel(
 
         def step_quantize(key):
             if key[0] == "y":
-                j, m0, width = units[key[1]]
+                j, m0, width = pieces[key[1]]
                 y_codes = work.tile([P, width], U32, name="y_codes", bufs=4, align_bytes=64)
-                quantize(grouped_of[key], y_codes[:], y_scales[PACK * j : P, m0 : m0 + width])
-                unstored.append((j, m0, width, y_codes))
+                quantize(grouped_of[key], y_codes[:], y_scales[SCALE_ROWS * j : P, m0 : m0 + width])
+                unstored_codes.append((j, m0, width, y_codes))
             else:
                 codes[key] = kept([P, CHUNK], U32, "codes_%s%d_%d" % key)
                 scales[key] = kept([P, CHUNK], U8, "scales_%s%d_%d" % key)
                 quantize(grouped_of[key], codes[key][:], scales[key][:])
 
-        def store_codes(count):
-            for j, m0, width, y_codes in unstored[:count]:
-                nc.sync.dma_start(
-                    out=out_1[j].rearrange("p m t -> p (m t)")[:, PACK * m0 : PACK * (m0 + width)].bitcast(I32),
-                    in_=y_codes[:].bitcast(I32),
-                )
-                if j == N_GROUPS - 1 and (m0 + width) % CHUNK == 0:
-                    store_scales(m0 + width - CHUNK, m0 + width)
-            unstored[:count] = []
-
-        def staggered(keys):
-            steps = [(step_interleave, keys[0])]
-            for before, key in zip(keys, keys[1:]):
-                steps.extend([(step_interleave, key), (step_quantize, before)])
-            return steps + [(step_quantize, keys[-1])]
-
-        steps = staggered(
-            [("w", 0, 0), ("w", 1, 0), ("h", 0, 0), ("w", 2, 0), ("h", 0, 1), ("w", 0, 1), ("h", 0, 2), ("w", 1, 1), ("w", 2, 1), ("h", 1, 0), ("h", 1, 1), ("h", 1, 2), ("h", 2, 0), ("h", 2, 1), ("h", 2, 2)]
-        ) + [
-            (fn, key)
-            for key in [] + [("y", u, 0) for u in range(len(units))]
-            for fn in (step_interleave, step_quantize)
-        ]
+        w_keys = [("w", g, j) for j in range(N_GROUPS) for g in range(F_GROUPS)]
+        h_keys = [("h", c, g) for c in range(CHUNKS) for g in range(F_GROUPS)]
+        operands = w_keys[:1]
+        for w_key, h_key in zip(w_keys[1 : 1 + F_GROUPS], h_keys[:F_GROUPS]):
+            operands.extend([w_key, h_key])
+        operands.extend(w_keys[1 + F_GROUPS :] + h_keys[F_GROUPS:])
+        steps = [(step_interleave, operands[0])]
+        for before, after in zip(operands, operands[1:]):
+            steps.extend([(step_interleave, after), (step_quantize, before)])
+        steps.append((step_quantize, operands[-1]))
+        for u in range(len(pieces)):
+            steps.extend([(step_interleave, ("y", u, 0)), (step_quantize, ("y", u, 0))])
 
         def run_steps(count):
-            for fn, key in steps[:count]:
+            for step, key in steps[:count]:
                 if key[0] == "y" and key[1] not in finished:
                     break
-                fn(key)
-                steps.remove((fn, key))
+                step(key)
+                steps.remove((step, key))
 
-        b1_slots = kept([P, PACK, P], BF16, "b1_slots")
+        b1_slots = kept([P, SLOTS, P], BF16, "b1_slots")
         nc.vector.tensor_copy(
-            out=b1_slots[:].rearrange("g t (a b) -> g t a b", b=4),
-            in_=b1_rows[:].rearrange("g (a t b) -> g t a b", t=PACK, b=4),
+            out=b1_slots[:].rearrange("g t (a b) -> g t a b", b=RUN),
+            in_=b1_rows[:].rearrange("g (a t b) -> g t a b", t=SLOTS, b=RUN),
         )
-        b1_ps = psum.tile([P, PACK, P], BF16, name="b1_ps", tag="bank")
-        for t in range(PACK):
+        b1_ps = psum.tile([P, SLOTS, P], BF16, name="b1_ps", tag="bank")
+        for t in range(SLOTS):
             nc.tensor.transpose(b1_ps[:, t, :], b1_slots[:, t, :], ident_bf[:])
-        b1_col = kept([P, PACK, F_GROUPS], F32, "b1_col")
+        b1_col = kept([P, SLOTS, F_GROUPS], F32, "b1_col")
         nc.scalar.copy(out=b1_col[:], in_=b1_ps[:, :, 0:F_GROUPS])
 
-        sort_w1(0)
-        sort_w1(1)
-        sort_w1(2)
+        w1w = [kept([P, K_PASSES, SLOTS, 2 * P], U8, "w1w%d" % g) for g in range(F_GROUPS)]
+        w1s = [kept([P, K_PASSES, SLOTS, P], U8, "w1s%d" % g) for g in range(F_GROUPS)]
+        for g in range(F_GROUPS):
+            nc.vector.tensor_copy(
+                out=w1s[g][:].bitcast(I32),
+                in_=w1s_raw[:, :, GROUP * g : GROUP * (g + 1)].bitcast(I32).rearrange("p k (a t) -> p k t a", t=SLOTS),
+            )
+            nc.vector.tensor_copy(
+                out=w1w[g][:].bitcast(I32).rearrange("p k t (a w) -> p k t a w", w=2),
+                in_=w1_raw[g].bitcast(I32).rearrange("p k (a t w) -> p k t a w", t=SLOTS, w=2),
+            )
+
         for c in range(CHUNKS):
             for g in range(F_GROUPS):
-                h_raw[c, g] = kept([P, PACK, CHUNK], BF16, "h_raw%d_%d" % (c, g))
-                for t in range(PACK):
+                h_raw[c, g] = kept([P, SLOTS, CHUNK], BF16, "h_raw%d_%d" % (c, g))
+                for t in range(SLOTS):
                     bank = psum.tile([P, CHUNK], F32, name="bank", tag="bank")
                     for k in range(K_PASSES):
                         nc.tensor.matmul_mx(
@@ -241,10 +223,17 @@ def tile_critic_value_contributions_h2_kernel(
                     nc.scalar.activation(
                         out=h_raw[c, g][:, t, :], in_=bank[:], func=ACT.Relu, bias=b1_col[:, t, g : g + 1]
                     )
-        run_steps(21)
+        run_steps(STEPS_BEFORE_CONSTANTS)
+        gain_col = kept([P, N_GROUPS, SLOTS], F32, "gain_col")
+        offset_col = kept([P, N_GROUPS, SLOTS], F32, "offset_col")
+        nc.scalar.copy(out=gain_col[:], in_=vw_col[:])
+        nc.vector.scalar_tensor_tensor(
+            out=offset_col[:], in0=base_col[:], scalar=-1.0, in1=vw_col[:], op0=ALU.mult, op1=ALU.mult
+        )
+        run_steps(STEPS_IN_LAYER_1 - STEPS_BEFORE_CONSTANTS)
 
-        def second(u, t):
-            j, m0, width = units[u]
+        def second_layer(u, t):
+            j, m0, width = pieces[u]
             c, lo = divmod(m0, CHUNK)
             bank = psum.tile([P, width], F32, name="bank", tag="bank")
             for g in range(F_GROUPS):
@@ -257,51 +246,61 @@ def tile_critic_value_contributions_h2_kernel(
                     start=(g == 0),
                     stop=(g == F_GROUPS - 1),
                 )
-            nc.scalar.activation(out=y[u][:, t, :], in_=bank[:], func=ACT.Relu, bias=b2_col[:, j, t : t + 1])
-            nc.vector.tensor_scalar(
-                out=y[u][:, t, :], in0=y[u][:, t, :],
-                scalar1=base_col[:, j, t : t + 1], scalar2=vw_col[:, j, t : t + 1],
-                op0=ALU.subtract, op1=ALU.mult,
-            )
+            slot = y[u][:, t, :]
+            nc.scalar.activation(out=slot, in_=bank[:], func=ACT.Relu, bias=b2_col[:, j, t : t + 1])
+            gain, offset = gain_col[:, j, t : t + 1], offset_col[:, j, t : t + 1]
+            if u < len(SCALAR_SLOTS) and t >= SLOTS - SCALAR_SLOTS[u]:
+                nc.scalar.activation(out=slot, in_=slot, func=ACT.Identity, scale=gain, bias=offset)
+            else:
+                nc.vector.tensor_scalar(out=slot, in0=slot, scalar1=gain, scalar2=offset, op0=ALU.mult, op1=ALU.add)
 
-        turned = []
-
-        def turn(u):
-            j, m0, width = units[u]
+        def transpose_piece(u):
+            j, m0, width = pieces[u]
+            turned = []
             for i in range(width // P):
-                bank = psum.tile([P, PACK, P], F32, name="bank", tag="bank")
-                for t in range(PACK):
+                bank = psum.tile([P, SLOTS, P], F32, name="bank", tag="bank")
+                for t in range(SLOTS):
                     nc.tensor.transpose(bank[:, t, :], y[u][:, t, P * i : P * (i + 1)], ident[:])
                 turned.append((bank, m0 + P * i, j))
+            return turned
 
-        def store_rows(count, copy):
-            for bank, m0, j in turned[:count]:
+        def store_rows(turned):
+            for bank, m0, j in turned:
                 rows = work.tile([P, GROUP], F32, name="rows", bufs=6)
-                copy(out=rows[:].rearrange("m (p t) -> m p t", t=PACK), in_=bank[:].rearrange("m t p -> m p t"))
-                nc.sync.dma_start(out=out_0[m0 : m0 + P, GROUP * j : GROUP * (j + 1)], in_=rows[:])
-            turned[:count] = []
-
-        def store_scales(m0, m1):
-            for q in range(QUADS):
-                nc.sync.dma_start(
-                    out=out_2[:, 4 * q : 4 * q + 4, m0:m1].bitcast(I32),
-                    in_=y_scales[32 * q : 32 * q + 4 * N_GROUPS, m0:m1].bitcast(I32),
+                nc.scalar.copy(
+                    out=rows[:].rearrange("m (p t) -> m p t", t=SLOTS), in_=bank[:].rearrange("m t p -> m p t")
                 )
+                nc.sync.dma_start(out=out_0[m0 : m0 + P, GROUP * j : GROUP * (j + 1)], in_=rows[:])
 
-        for u in range(len(units)):
-            y[u] = work.tile([P, PACK, units[u][2]], F32, name="y", bufs=6, align_bytes=64)
-            for t in range(PACK):
-                second(u, t)
+        def store_planes():
+            for j, m0, width, y_codes in unstored_codes:
+                m1 = m0 + width
+                nc.sync.dma_start(
+                    out=out_1[j].rearrange("p m t -> p (m t)")[:, SLOTS * m0 : SLOTS * m1].bitcast(I32),
+                    in_=y_codes[:].bitcast(I32),
+                )
+                if j == N_GROUPS - 1 and m1 % CHUNK == 0:
+                    for q in range(P // QUADRANT):
+                        live = y_scales[QUADRANT * q : QUADRANT * q + SCALE_ROWS * N_GROUPS, m1 - CHUNK : m1]
+                        nc.sync.dma_start(
+                            out=out_2[:, SCALE_ROWS * q : SCALE_ROWS * (q + 1), m1 - CHUNK : m1].bitcast(I32),
+                            in_=live.bitcast(I32),
+                        )
+            unstored_codes.clear()
+
+        last = len(pieces) - 1
+        for u in range(len(pieces)):
+            y[u] = work.tile([P, SLOTS, pieces[u][2]], F32, name="y", bufs=6, align_bytes=64)
+            for t in range(SLOTS):
+                second_layer(u, t)
                 if t == 0:
                     finished.add(u - 1)
                 run_steps(1)
             if u > 0:
-                turn(u - 1)
-                store_rows(4, nc.scalar.copy)
-                store_codes(max(len(unstored) - 0, 0))
-        turn(len(units) - 1)
-        finished.add(len(units) - 1)
-        store_codes(len(unstored))
-        store_rows(2, nc.scalar.copy)
+                store_rows(transpose_piece(u - 1))
+                store_planes()
+        turned_last = transpose_piece(last)
+        finished.add(last)
+        store_rows(turned_last)
         run_steps(len(steps))
-        store_codes(len(unstored))
+        store_planes()

from contextlib import ExitStack

import concourse.mybir as mybir
from concourse.masks import make_identity

M, K, F, N = 1536, 1024, 1536, 1024
FLOPS = 2 * M * K * F + 2 * M * F * N

F32 = mybir.dt.float32
BF16 = mybir.dt.bfloat16
I32 = mybir.dt.int32
U32 = mybir.dt.uint32
U8 = mybir.dt.uint8
FP8X4 = mybir.dt.float8_e4m3fn_x4
FP4X4 = mybir.dt.float4_e2m1fn_x4
ACT = mybir.ActivationFunctionType
ALU = mybir.AluOpType

P = 128
SLOTS = 4
GROUP = P * SLOTS
RUN = 4
CHUNK = 512
K_PASSES = K // GROUP
F_GROUPS = F // GROUP
N_GROUPS = N // GROUP
CHUNKS = M // CHUNK
QUADRANT = 32
SCALE_ROWS = 4
QUADRANT_ORDER = (0, 2, 1, 3)
STEPS_IN_LAYER_1 = 21
STEPS_BEFORE_CONSTANTS = 12
SCALAR_SLOTS = (2, 1, 1)


def tile_critic_value_contributions_h2_kernel(
    tc, x_words, x_scales, w1_words, w1_scales, b1, w2, b2, baseline, value_w, out_0, out_1, out_2
):
    nc = tc.nc
    with ExitStack() as ctx:
        keep = ctx.enter_context(tc.tile_pool(name="keep", bufs=1))
        work = ctx.enter_context(tc.tile_pool(name="work", bufs=3))
        psum = ctx.enter_context(tc.psum_pool(name="psum", bufs=8))
        ctx.enter_context(tc.manual_schedule())

        def kept(shape, dtype, name):
            return keep.tile(shape, dtype, name=name, align_bytes=64)

        w1s_raw = kept([P, K_PASSES, F], U8, "w1s_raw")
        xs_first = kept([P, K_PASSES, CHUNK], U8, "xs_first")
        xs_rest = kept([P, K_PASSES, M - CHUNK], U8, "xs_rest")
        b1_rows = kept([P, GROUP], BF16, "b1_rows")
        nc.vector.memset(b1_rows[:], 0.0)
        nc.vector.memset(w1s_raw[:].bitcast(I32), 0)
        nc.vector.memset(xs_first[:].bitcast(I32), 0)
        nc.vector.memset(xs_rest[:].bitcast(I32), 0)
        xs = [xs_first[:]] + [xs_rest[:, :, CHUNK * c : CHUNK * (c + 1)] for c in range(CHUNKS - 1)]

        w1_first = kept([P, K_PASSES, 2 * GROUP], U8, "w1_first")
        w1_rest = kept([P, K_PASSES, 2 * (F - GROUP)], U8, "w1_rest")
        w1_raw = [w1_first[:]] + [w1_rest[:, :, 2 * GROUP * g : 2 * GROUP * (g + 1)] for g in range(F_GROUPS - 1)]
        xw = [kept([P, K_PASSES, CHUNK], U32, "xw%d" % c) for c in range(CHUNKS)]
        w2_raw = {
            (g, j): kept([P, SLOTS, GROUP], BF16, "w2_raw%d_%d" % (g, j))
            for g in range(F_GROUPS)
            for j in range(N_GROUPS)
        }

        def load_scales(plane, rows, lo, hi):
            for q in QUADRANT_ORDER:
                nc.sync.dma_start(
                    out=plane[QUADRANT * q : QUADRANT * q + SCALE_ROWS, :, :].bitcast(I32),
                    in_=rows[:, SCALE_ROWS * q : SCALE_ROWS * (q + 1), lo:hi].rearrange("k r n -> r k n").bitcast(I32),
                )

        def load_w1(engine, dst, f0, f1):
            engine.dma_start(
                out=dst[:].bitcast(I32),
                in_=w1_words[:, :, 2 * f0 : 2 * f1].rearrange("k p n -> p k n").bitcast(I32),
            )

        def load_x(c):
            words = x_words.rearrange("k p n t -> p k (n t)")
            nc.sync.dma_start(
                out=xw[c][:].bitcast(I32), in_=words[:, :, SLOTS * CHUNK * c : SLOTS * CHUNK * (c + 1)].bitcast(I32)
            )

        def load_w2(g, j):
            rows = w2[GROUP * g : GROUP * (g + 1), GROUP * j : GROUP * (j + 1)]
            rows = rows.rearrange("(a t b) n -> b a t n", t=SLOTS, b=RUN)
            for b in range(RUN):
                nc.sync.dma_start(out=w2_raw[g, j][b:P:RUN, :, :], in_=rows[b])

        ident = kept([P, P], F32, "ident")
        make_identity(nc, ident[:])
        ident_bf = kept([P, P], BF16, "ident_bf")
        load_w1(nc.scalar, w1_first, 0, GROUP)
        nc.scalar.dma_start(out=b1_rows[0:F_GROUPS, :], in_=b1.rearrange("(g f) -> g f", g=F_GROUPS))
        nc.scalar.activation(out=ident_bf[:], in_=ident[:], func=ACT.Relu)
        load_scales(w1s_raw, w1_scales, 0, F)
        load_x(0)
        load_scales(xs_first, x_scales, 0, CHUNK)
        load_w1(nc.sync, w1_rest, GROUP, F)
        for g in range(F_GROUPS):
            load_w2(g, 0)
        load_scales(xs_rest, x_scales, CHUNK, M)
        load_x(1)
        for g in range(F_GROUPS):
            load_w2(g, 1)
        load_x(2)
        unit_cols = []
        for name, vec in (("b2_col", b2), ("base_col", baseline), ("vw_col", value_w)):
            col = kept([P, N_GROUPS, SLOTS], BF16, name)
            nc.sync.dma_start(out=col[:], in_=vec.rearrange("(j p t) -> p j t", p=P, t=SLOTS))
            unit_cols.append(col)
        b2_col, base_col, vw_col = unit_cols

        codes = {}
        scales = {}
        h_raw = {}
        y = {}
        grouped_of = {}
        unstored_codes = []
        finished = set()
        y_scales = kept([P, M], U8, "y_scales")
        half = CHUNK // 2
        pieces = [(j, CHUNK * c, CHUNK) for c in range(CHUNKS) for j in range(N_GROUPS)]
        pieces = pieces[:-1] + [(N_GROUPS - 1, M - CHUNK, half), (N_GROUPS - 1, M - half, half)]

        def interleave(src, width, pattern, **sizes):
            grouped = work.tile([P, SLOTS * width], BF16, name="grouped", align_bytes=64)
            nc.vector.tensor_copy(out=grouped[:].rearrange(pattern, **sizes), in_=src)
            return grouped

        def interleave_slots(src):
            walk = src[:].rearrange("p t (c i) -> p c t i", i=4)
            return interleave(walk, src.shape[2], "p (c i t) -> p c t i", i=4, t=SLOTS)

        def interleave_w2(g, j):
            walk = w2_raw[g, j][:].rearrange("p s (c i t) -> p t c s i", i=2, t=SLOTS)
            return interleave(walk, GROUP, "p (t c i s) -> p t c s i", t=SLOTS, i=2, s=SLOTS)

        def quantize(grouped, words, plane):
            nc.vector.quantize_mx(out=words.bitcast(FP8X4), scales=plane, in_=grouped[:])

        def step_interleave(key):
            if key[0] == "w":
                grouped_of[key] = interleave_w2(key[1], key[2])
            elif key[0] == "h":
                grouped_of[key] = interleave_slots(h_raw[key[1], key[2]])
            else:
                grouped_of[key] = interleave_slots(y[key[1]])

        def step_quantize(key):
            if key[0] == "y":
                j, m0, width = pieces[key[1]]
                y_codes = work.tile([P, width], U32, name="y_codes", bufs=4, align_bytes=64)
                quantize(grouped_of[key], y_codes[:], y_scales[SCALE_ROWS * j : P, m0 : m0 + width])
                unstored_codes.append((j, m0, width, y_codes))
            else:
                codes[key] = kept([P, CHUNK], U32, "codes_%s%d_%d" % key)
                scales[key] = kept([P, CHUNK], U8, "scales_%s%d_%d" % key)
                quantize(grouped_of[key], codes[key][:], scales[key][:])

        w_keys = [("w", g, j) for j in range(N_GROUPS) for g in range(F_GROUPS)]
        h_keys = [("h", c, g) for c in range(CHUNKS) for g in range(F_GROUPS)]
        operands = w_keys[:1]
        for w_key, h_key in zip(w_keys[1 : 1 + F_GROUPS], h_keys[:F_GROUPS]):
            operands.extend([w_key, h_key])
        operands.extend(w_keys[1 + F_GROUPS :] + h_keys[F_GROUPS:])
        steps = [(step_interleave, operands[0])]
        for before, after in zip(operands, operands[1:]):
            steps.extend([(step_interleave, after), (step_quantize, before)])
        steps.append((step_quantize, operands[-1]))
        for u in range(len(pieces)):
            steps.extend([(step_interleave, ("y", u, 0)), (step_quantize, ("y", u, 0))])

        def run_steps(count):
            for step, key in steps[:count]:
                if key[0] == "y" and key[1] not in finished:
                    break
                step(key)
                steps.remove((step, key))

        b1_slots = kept([P, SLOTS, P], BF16, "b1_slots")
        nc.vector.tensor_copy(
            out=b1_slots[:].rearrange("g t (a b) -> g t a b", b=RUN),
            in_=b1_rows[:].rearrange("g (a t b) -> g t a b", t=SLOTS, b=RUN),
        )
        b1_ps = psum.tile([P, SLOTS, P], BF16, name="b1_ps", tag="bank")
        for t in range(SLOTS):
            nc.tensor.transpose(b1_ps[:, t, :], b1_slots[:, t, :], ident_bf[:])
        b1_col = kept([P, SLOTS, F_GROUPS], F32, "b1_col")
        nc.scalar.copy(out=b1_col[:], in_=b1_ps[:, :, 0:F_GROUPS])

        w1w = [kept([P, K_PASSES, SLOTS, 2 * P], U8, "w1w%d" % g) for g in range(F_GROUPS)]
        w1s = [kept([P, K_PASSES, SLOTS, P], U8, "w1s%d" % g) for g in range(F_GROUPS)]
        for g in range(F_GROUPS):
            nc.vector.tensor_copy(
                out=w1s[g][:].bitcast(I32),
                in_=w1s_raw[:, :, GROUP * g : GROUP * (g + 1)].bitcast(I32).rearrange("p k (a t) -> p k t a", t=SLOTS),
            )
            nc.vector.tensor_copy(
                out=w1w[g][:].bitcast(I32).rearrange("p k t (a w) -> p k t a w", w=2),
                in_=w1_raw[g].bitcast(I32).rearrange("p k (a t w) -> p k t a w", t=SLOTS, w=2),
            )

        for c in range(CHUNKS):
            for g in range(F_GROUPS):
                h_raw[c, g] = kept([P, SLOTS, CHUNK], BF16, "h_raw%d_%d" % (c, g))
                for t in range(SLOTS):
                    bank = psum.tile([P, CHUNK], F32, name="bank", tag="bank")
                    for k in range(K_PASSES):
                        nc.tensor.matmul_mx(
                            out=bank[:],
                            lhsT=w1w[g][:, k, t, :].bitcast(FP4X4),
                            lhsT_scale=w1s[g][:, k, t, :],
                            rhs=xw[c][:, k, :].bitcast(FP8X4),
                            rhs_scale=xs[c][:, k, :],
                            start=(k == 0),
                            stop=(k == K_PASSES - 1),
                        )
                    nc.scalar.activation(
                        out=h_raw[c, g][:, t, :], in_=bank[:], func=ACT.Relu, bias=b1_col[:, t, g : g + 1]
                    )
        run_steps(STEPS_BEFORE_CONSTANTS)
        gain_col = kept([P, N_GROUPS, SLOTS], F32, "gain_col")
        offset_col = kept([P, N_GROUPS, SLOTS], F32, "offset_col")
        nc.scalar.copy(out=gain_col[:], in_=vw_col[:])
        nc.vector.scalar_tensor_tensor(
            out=offset_col[:], in0=base_col[:], scalar=-1.0, in1=vw_col[:], op0=ALU.mult, op1=ALU.mult
        )
        run_steps(STEPS_IN_LAYER_1 - STEPS_BEFORE_CONSTANTS)

        def second_layer(u, t):
            j, m0, width = pieces[u]
            c, lo = divmod(m0, CHUNK)
            bank = psum.tile([P, width], F32, name="bank", tag="bank")
            for g in range(F_GROUPS):
                nc.tensor.matmul_mx(
                    out=bank[:],
                    lhsT=codes["w", g, j][:, P * t : P * (t + 1)].bitcast(FP8X4),
                    lhsT_scale=scales["w", g, j][:, P * t : P * (t + 1)],
                    rhs=codes["h", c, g][:, lo : lo + width].bitcast(FP8X4),
                    rhs_scale=scales["h", c, g][:, lo : lo + width],
                    start=(g == 0),
                    stop=(g == F_GROUPS - 1),
                )
            slot = y[u][:, t, :]
            nc.scalar.activation(out=slot, in_=bank[:], func=ACT.Relu, bias=b2_col[:, j, t : t + 1])
            gain, offset = gain_col[:, j, t : t + 1], offset_col[:, j, t : t + 1]
            if u < len(SCALAR_SLOTS) and t >= SLOTS - SCALAR_SLOTS[u]:
                nc.scalar.activation(out=slot, in_=slot, func=ACT.Identity, scale=gain, bias=offset)
            else:
                nc.vector.tensor_scalar(out=slot, in0=slot, scalar1=gain, scalar2=offset, op0=ALU.mult, op1=ALU.add)

        def transpose_piece(u):
            j, m0, width = pieces[u]
            turned = []
            for i in range(width // P):
                bank = psum.tile([P, SLOTS, P], F32, name="bank", tag="bank")
                for t in range(SLOTS):
                    nc.tensor.transpose(bank[:, t, :], y[u][:, t, P * i : P * (i + 1)], ident[:])
                turned.append((bank, m0 + P * i, j))
            return turned

        def store_rows(turned):
            for bank, m0, j in turned:
                rows = work.tile([P, GROUP], F32, name="rows", bufs=6)
                nc.scalar.copy(
                    out=rows[:].rearrange("m (p t) -> m p t", t=SLOTS), in_=bank[:].rearrange("m t p -> m p t")
                )
                nc.sync.dma_start(out=out_0[m0 : m0 + P, GROUP * j : GROUP * (j + 1)], in_=rows[:])

        def store_planes():
            for j, m0, width, y_codes in unstored_codes:
                m1 = m0 + width
                nc.sync.dma_start(
                    out=out_1[j].rearrange("p m t -> p (m t)")[:, SLOTS * m0 : SLOTS * m1].bitcast(I32),
                    in_=y_codes[:].bitcast(I32),
                )
                if j == N_GROUPS - 1 and m1 % CHUNK == 0:
                    for q in range(P // QUADRANT):
                        live = y_scales[QUADRANT * q : QUADRANT * q + SCALE_ROWS * N_GROUPS, m1 - CHUNK : m1]
                        nc.sync.dma_start(
                            out=out_2[:, SCALE_ROWS * q : SCALE_ROWS * (q + 1), m1 - CHUNK : m1].bitcast(I32),
                            in_=live.bitcast(I32),
                        )
            unstored_codes.clear()

        last = len(pieces) - 1
        for u in range(len(pieces)):
            y[u] = work.tile([P, SLOTS, pieces[u][2]], F32, name="y", bufs=6, align_bytes=64)
            for t in range(SLOTS):
                second_layer(u, t)
                if t == 0:
                    finished.add(u - 1)
                run_steps(1)
            if u > 0:
                store_rows(transpose_piece(u - 1))
                store_planes()
        turned_last = transpose_piece(last)
        finished.add(last)
        store_rows(turned_last)
        run_steps(len(steps))
        store_planes()
